import numpy as np
import ml_dtypes


def mxq(x, axis, fmt="e4m3"):
    dtype, down = {"e4m3": (ml_dtypes.float8_e4m3fn, 7), "e5m2": (ml_dtypes.float8_e5m2, 14)}[fmt]
    v = np.moveaxis(np.asarray(x, np.float32).astype(ml_dtypes.bfloat16).astype(np.float64), axis, -1)
    blocks = v.reshape(v.shape[:-1] + (-1, 32))
    amax = np.abs(blocks).max(-1, keepdims=True)
    byte = np.maximum(np.where(amax > 0, np.frexp(amax)[1] - 1 + 127, 0) - down, 1)
    scale = np.exp2(byte - 127.0)
    codes = (blocks / scale).astype(np.float32).astype(dtype).astype(np.float64)
    return np.moveaxis((codes * scale).reshape(v.shape), -1, axis)


WIDE = False


def mx_kscale(k):
    if not WIDE:
        return np.ones(k)
    levels = np.array([10, -10, 5, -5, 0])
    if k % 512:
        return np.exp2(np.random.permutation(np.resize(levels, k // 32))).repeat(32)
    a = np.empty((k // 512, 16))
    for p in range(k // 512):
        a[p, :8] = np.random.permutation(np.resize(levels, 8))
        for g in range(8):
            far = levels[np.abs(levels - a[p, g]) >= 10]
            a[p, g + 8] = far[np.random.randint(len(far))]
    return np.exp2(a.ravel()).repeat(32)


def f64(x):
    return np.asarray(x).astype(np.float64)


def striped(idx):
    return np.tile(idx.reshape(-1, 16).T, (8, 1)).astype(np.uint16)


def unstriped(offs):
    return offs[:16].T.reshape(-1).astype(np.int64)


def striped8(idx):
    return np.concatenate([x.reshape(-1, 16).T for x in idx]).astype(np.uint16)


def runs(offs, k):
    lists = np.stack([offs[16 * r : 16 * r + 16].T.reshape(-1) for r in range(8)]).astype(np.int64)
    return lists[np.arange(k) % 512 // 64]


def pack_weight(w):
    k, n = w.shape
    w = f64(np.asarray(w, np.float32).astype(ml_dtypes.bfloat16)).reshape(k // 32, 32, n)
    amax = np.abs(w).max(1)
    byte = np.clip(np.where(amax > 0, np.frexp(amax)[1] - 1 + 127 - 7, 1), 1, 254)
    scaled = (w * np.exp2(127.0 - byte)[:, None, :]).reshape(k, n).astype(np.float32)
    words = np.ascontiguousarray(scaled.reshape(k // 512, 128, 4, n).transpose(0, 1, 3, 2)).astype(ml_dtypes.float8_e4m3fn).view(np.uint8)
    return words, np.ascontiguousarray(byte.astype(np.uint8).reshape(k // 512, 16, n))


def unpack_weight(words, scales):
    g, p, n, _ = words.shape
    vals = np.ascontiguousarray(words).view(ml_dtypes.float8_e4m3fn).astype(np.float64) * np.repeat(np.exp2(scales.astype(np.float64) - 127.0), 8, axis=1)[..., None]
    return vals.transpose(0, 1, 3, 2).reshape(g * 512, n)


def sigmoid(v):
    return 1.0 / (1.0 + np.exp(-np.maximum(v, -700.0)))


K, T, S, N, H, C = 512, 2048, 512, 512, 512, 512


def setup_inputs():
    n = np.random.standard_normal
    s = mx_kscale(K)[:, None]
    u = mx_kscale(S)
    packed_xT = pack_weight(n((K, T)) * s)
    return {
        "x_words": packed_xT[0],
        "x_scales": packed_xT[1],
        "w1": (n((K, H)) / np.sqrt(K) / s).astype(np.float32),
        "w2": (n((K, H)) / np.sqrt(K) / s).astype(np.float32),
        "gn": (np.random.uniform(0.5, 1.5, (H, 1)) * u[:, None]).astype(np.float32),
        "w3": (n((H, N)) / np.sqrt(H) / u[:, None]).astype(np.float32),
        "gs": (np.random.uniform(0.5, 1.5, (K, 1)) / s).astype(np.float32),
        "offs": striped(np.random.permutation(T)[:S]),
        "two": striped(np.random.permutation(T)[:S]),
        "n1": striped(np.random.permutation(S)),
        "n2": striped(np.random.permutation(S)),
        "n3": striped(np.random.permutation(S)),
        "n4": striped(np.random.permutation(S)),
        "n5": striped8(np.stack([np.random.permutation(S) for _ in range(8)])),
        "n6": striped8(np.stack([np.random.permutation(S) for _ in range(8)])),
        "cand": striped(np.random.permutation(T)[:C]),
        "n7": striped(np.random.permutation(S)),
        "n8": striped(np.random.permutation(S)),
        "n9": striped(np.random.permutation(S)),
    }


def reference(x_words, x_scales, w1, w2, gn, w3, gs, offs, two, n1, n2, n3, n4, n5, n6, cand, n7, n8, n9):
    x_cand = unpack_weight(x_words, x_scales)[:, unstriped(cand)]
    x_two = unpack_weight(x_words, x_scales)[:, unstriped(two)]
    d = mxq(f64(w2), 0, "e4m3").T @ x_two
    z2 = f64(gs) * (d * (sigmoid(d[np.arange(H)[:, None], runs(n5, H)] - (d[np.arange(H)[:, None], runs(n6, H)]))))
    b = 0.0625 * ((x_cand.T @ mxq(z2, 0, "e4m3")))
    xq = unpack_weight(x_words, x_scales)[:, unstriped(offs)]
    y = mxq(f64(w1), 0, "e4m3").T @ xq
    z = f64(gn) * (0.75 * (y[:, unstriped(n1)] * y[:, unstriped(n2)] - (y[:, unstriped(n3)] * y[:, unstriped(n4)])))
    a = mxq(f64(w3), 0, "e4m3").T @ mxq(z, 0, "e4m3")
    return b * (a[:, unstriped(n7)] - a) + 0.5 * (b[:, unstriped(n9)] * (a[:, unstriped(n8)] - a))

@@ -1,0 +1,251 @@
+from contextlib import ExitStack
+
+import concourse.mybir as mybir
+
+K, T, S, N, H, C = 512, 2048, 512, 512, 512, 512
+FLOPS = 4 * 2 * 512 * 512 * 512
+
+F32 = mybir.dt.float32
+BF16 = mybir.dt.bfloat16
+I32 = mybir.dt.int32
+U32 = mybir.dt.uint32
+U16 = mybir.dt.uint16
+U8 = mybir.dt.uint8
+FP8X4 = mybir.dt.float8_e4m3fn_x4
+ALU = mybir.AluOpType
+ACT = mybir.ActivationFunctionType
+
+P = 128
+PACK = 4
+HALF = S // 2
+LIST_COLS = S // 16
+
+
+def tile_picked_tfcdflowbdetcmp_none_p_kernel(
+    tc, x_words, x_scales, w1, w2, gn, w3, gs, offs, two, n1, n2, n3, n4, n5, n6, cand, n7, n8, n9, out
+):
+    nc = tc.nc
+    with ExitStack() as ctx:
+        lists = ctx.enter_context(tc.tile_pool(name="lists", bufs=1))
+        keep = ctx.enter_context(tc.tile_pool(name="keep", bufs=1))
+        psum = ctx.enter_context(tc.psum_pool(name="psum", bufs=1))
+
+        def load_list(name, src):
+            tile = lists.tile([P, LIST_COLS], U16, name=name)
+            nc.sync.dma_start(tile[:], src)
+            return tile
+
+        def plane(name):
+            return keep.tile([P, S], F32, name=name, align_bytes=64)
+
+        def half_cols(h):
+            return slice(h * HALF, (h + 1) * HALF)
+
+        def looked_up(window, lst, h):
+            return window[:].indirect(lst[:, h * LIST_COLS // 2 : (h + 1) * LIST_COLS // 2])
+
+        scale_rows = keep.tile([P, T], U8, name="scale_rows", align_bytes=64)
+        nc.vector.memset(scale_rows[:].bitcast(I32), 0)
+        for q in range(4):
+            nc.scalar.dma_start(
+                out=scale_rows[32 * q : 32 * q + 4, :].bitcast(I32), in_=x_scales[0, 4 * q : 4 * q + 4, :].bitcast(I32)
+            )
+        l_offs = load_list("l_offs", offs)
+        l_two = load_list("l_two", two)
+        words = keep.tile([P, T], I32, name="words", align_bytes=64)
+        nc.sync.dma_start(out=words[:], in_=x_words[0].rearrange("p n t -> p (n t)").bitcast(I32))
+        w1_raw = []
+        for h in range(2):
+            raw = keep.tile([P, PACK, H // 2], F32, name="w1_raw%d" % h, align_bytes=64)
+            nc.sync.dma_start(out=raw[:], in_=w1.rearrange("(p j) c -> p j c", j=PACK)[:, :, h * 256 : (h + 1) * 256])
+            w1_raw.append(raw)
+        l_n1 = load_list("l_n1", n1)
+        l_n3 = load_list("l_n3", n3)
+        w2_raw = keep.tile([P, PACK, H], F32, name="w2_raw", align_bytes=64)
+        nc.sync.dma_start(out=w2_raw[:], in_=w2.rearrange("(p j) c -> p j c", j=PACK))
+        gn_sb = keep.tile([P, PACK], F32, name="gn_sb")
+        nc.sync.dma_start(out=gn_sb[:], in_=gn.rearrange("(p t) o -> p (t o)", t=PACK))
+        l_n2 = load_list("l_n2", n2)
+        l_n4 = load_list("l_n4", n4)
+        l_cand = load_list("l_cand", cand)
+        w3_raw = keep.tile([P, PACK, N], F32, name="w3_raw", align_bytes=64)
+        nc.sync.dma_start(out=w3_raw[:], in_=w3.rearrange("(p j) c -> p j c", j=PACK))
+        l_n5 = load_list("l_n5", n5)
+        l_n6 = load_list("l_n6", n6)
+        gs_sb = keep.tile([P, PACK], F32, name="gs_sb")
+        nc.sync.dma_start(out=gs_sb[:], in_=gs.rearrange("(p t) o -> p (t o)", t=PACK))
+        l_n7 = load_list("l_n7", n7)
+        l_n8 = load_list("l_n8", n8)
+        l_n9 = load_list("l_n9", n9)
+
+        def mx_tiles(name):
+            codes = keep.tile([P, S], U32, name=name + "_codes", align_bytes=64)
+            scales = keep.tile([P, S], U8, name=name + "_scales", align_bytes=64)
+            return codes, scales
+
+        def pick_bytes(name, lst, tag):
+            picked = keep.tile([P, S], U8, name=name, tag=tag, align_bytes=64)
+            nc.vector.tensor_copy(out=picked[:], in_=scale_rows[:].indirect(lst[:]))
+            return picked
+
+        def pick_words(name, lst):
+            picked = keep.tile([P, S], U32, name=name, tag="picked_words", align_bytes=64)
+            nc.vector.tensor_copy(out=picked[:], in_=words[:].bitcast(U32).indirect(lst[:]))
+            return picked
+
+        def quantize(operand, grouped, first, count):
+            nc.vector.quantize_mx(
+                out=operand[0][:, first : first + count].bitcast(FP8X4),
+                scales=operand[1][:, first : first + count],
+                in_=grouped[:, PACK * first : PACK * (first + count)],
+            )
+
+        def product(bank, stationary, t, moving):
+            cols = slice(t * P, (t + 1) * P)
+            nc.tensor.matmul_mx(
+                out=bank[:],
+                lhsT=stationary[0][:, cols].bitcast(FP8X4),
+                lhsT_scale=stationary[1][:, cols],
+                rhs=moving[0][:].bitcast(FP8X4),
+                rhs_scale=moving[1][:],
+                start=True,
+                stop=True,
+            )
+
+        def interleaved(grouped, h):
+            cols = slice(h * HALF * PACK, (h + 1) * HALF * PACK)
+            return grouped[:, cols].rearrange("p (c i t) -> p c t i", i=2, t=PACK)
+
+        def by_pairs(planes, h):
+            return planes[:, :, half_cols(h)].rearrange("p t (c i) -> p c t i", i=2)
+
+        offs_bytes = pick_bytes("offs_bytes", l_offs, "picked_bytes")
+        x_offs = (pick_words("offs_words", l_offs), offs_bytes)
+        two_bytes = pick_bytes("two_bytes", l_two, "two_bytes")
+
+        w1_g = keep.tile([P, PACK * H], BF16, name="w1_g", align_bytes=64)
+        for h in range(2):
+            nc.scalar.copy(
+                out=w1_g[:].rearrange("p (t m j) -> p m j t", t=PACK, j=PACK)[:, h * 64 : (h + 1) * 64],
+                in_=w1_raw[h][:].rearrange("p j (m t) -> p m j t", t=PACK),
+            )
+        w1_q = mx_tiles("w1")
+        y_banks = []
+        for t in range(PACK):
+            quantize(w1_q, w1_g, t * P, P)
+            bank = psum.tile([P, S], F32, name="y_bank%d" % t, tag="ya%d" % t)
+            product(bank, w1_q, t, x_offs)
+            y_banks.append(bank)
+
+        x_two = (pick_words("two_words", l_two), two_bytes)
+        cand_bytes = pick_bytes("cand_bytes", l_cand, "picked_bytes")
+
+        prod12 = keep.tile([P, PACK, S], F32, name="prod12", align_bytes=64)
+        prod34 = keep.tile([P, PACK, S], F32, name="prod34", align_bytes=64)
+        w2_g = keep.tile([P, PACK * H], BF16, name="w2_g", align_bytes=64)
+        w2_q = mx_tiles("w2")
+        d_banks = []
+        for t in range(PACK):
+            y = plane("y%d" % t)
+            nc.scalar.copy(out=y[:], in_=y_banks[t][:])
+            yg = plane("yg%d" % t)
+            nc.vector.tensor_scalar(
+                out=yg[:], in0=y[:], scalar1=gn_sb[:, t : t + 1], scalar2=0.75, op0=ALU.mult, op1=ALU.mult
+            )
+            y1, y3 = plane("y1_%d" % t), plane("y3_%d" % t)
+            for h in range(2):
+                nc.scalar.activation(out=y1[:, half_cols(h)], in_=looked_up(y, l_n1, h), func=ACT.Copy)
+            for h in range(2):
+                nc.scalar.activation(out=y3[:, half_cols(h)], in_=looked_up(y, l_n3, h), func=ACT.Copy)
+            for h in range(2):
+                nc.vector.tensor_tensor(
+                    out=prod12[:, t, half_cols(h)], in0=looked_up(yg, l_n2, h), in1=y1[:, half_cols(h)], op=ALU.mult
+                )
+            for h in range(2):
+                nc.vector.tensor_tensor(
+                    out=prod34[:, t, half_cols(h)], in0=looked_up(yg, l_n4, h), in1=y3[:, half_cols(h)], op=ALU.mult
+                )
+            if t == 0:
+                nc.scalar.copy(
+                    out=w2_g[:].rearrange("p (t m j) -> p m j t", t=PACK, j=PACK),
+                    in_=w2_raw[:].rearrange("p j (m t) -> p m j t", t=PACK),
+                )
+                quantize(w2_q, w2_g, 0, H)
+                for td in range(PACK):
+                    bank = psum.tile([P, S], F32, name="d_bank%d" % td, tag="db%d" % td)
+                    product(bank, w2_q, td, x_two)
+                    d_banks.append(bank)
+                x_cand = (pick_words("cand_words", l_cand), cand_bytes)
+
+        w3_g = keep.tile([P, PACK * N], BF16, name="w3_g", align_bytes=64)
+        nc.vector.tensor_copy(
+            out=w3_g[:].rearrange("p (c i j) -> p c j i", i=4, j=PACK),
+            in_=w3_raw[:].rearrange("p j (c i) -> p c j i", i=4),
+        )
+        z_g = keep.tile([P, PACK * S], BF16, name="z_g", align_bytes=64)
+        for h in range(2):
+            nc.vector.tensor_tensor(
+                out=interleaved(z_g, h), in0=by_pairs(prod12, h), in1=by_pairs(prod34, h), op=ALU.subtract
+            )
+        w3_q = mx_tiles("w3")
+        quantize(w3_q, w3_g, 0, N)
+        z_q = mx_tiles("z")
+        quantize(z_q, z_g, 0, S)
+        a_banks = []
+        for t in range(PACK):
+            bank = psum.tile([P, S], F32, name="a_bank%d" % t, tag="ya%d" % t)
+            product(bank, w3_q, t, z_q)
+            a_banks.append(bank)
+
+        dg = keep.tile([P, PACK, S], F32, name="dg", align_bytes=64)
+        gate = keep.tile([P, PACK, S], F32, name="gate", align_bytes=64)
+        for t in range(PACK):
+            d = plane("d%d" % t)
+            nc.scalar.copy(out=d[:], in_=d_banks[t][:])
+            d5 = plane("d5_%d" % t)
+            for h in range(2):
+                nc.scalar.activation(out=d5[:, half_cols(h)], in_=looked_up(d, l_n5, h), func=ACT.Copy)
+            nc.vector.tensor_scalar(
+                out=dg[:, t, :], in0=d[:], scalar1=gs_sb[:, t : t + 1], scalar2=None, op0=ALU.mult
+            )
+            back = plane("back%d" % t)
+            for h in range(2):
+                nc.vector.tensor_tensor(
+                    out=back[:, half_cols(h)], in0=looked_up(d, l_n6, h), in1=d5[:, half_cols(h)], op=ALU.subtract
+                )
+            nc.scalar.activation(out=gate[:, t, :], in_=back[:], func=ACT.Sigmoid, scale=-1.0)
+        z2_g = keep.tile([P, PACK * S], BF16, name="z2_g", align_bytes=64)
+        for h in range(2):
+            nc.vector.tensor_tensor(out=interleaved(z2_g, h), in0=by_pairs(dg, h), in1=by_pairs(gate, h), op=ALU.mult)
+        z2_q = mx_tiles("z2")
+        quantize(z2_q, z2_g, 0, S)
+        b_banks = []
+        for t in range(PACK):
+            bank = psum.tile([P, S], F32, name="b_bank%d" % t, tag="db%d" % t)
+            product(bank, x_cand, t, z2_q)
+            b_banks.append(bank)
+
+        for t in range(PACK):
+            a = plane("a%d" % t)
+            nc.scalar.copy(out=a[:], in_=a_banks[t][:])
+            a7, a8 = plane("a7_%d" % t), plane("a8_%d" % t)
+            for h in range(2):
+                nc.scalar.activation(out=a7[:, half_cols(h)], in_=looked_up(a, l_n7, h), func=ACT.Copy)
+            for h in range(2):
+                nc.scalar.activation(out=a8[:, half_cols(h)], in_=looked_up(a, l_n8, h), func=ACT.Copy)
+            b = plane("b%d" % t)
+            nc.scalar.activation(out=b[:], in_=b_banks[t][:], func=ACT.Copy, scale=0.0625)
+            u, v = a7, a8
+            nc.vector.tensor_tensor(out=u[:], in0=a7[:], in1=a[:], op=ALU.subtract)
+            nc.vector.tensor_tensor(out=v[:], in0=a8[:], in1=a[:], op=ALU.subtract)
+            bu, bv = plane("bu%d" % t), plane("bv%d" % t)
+            nc.vector.tensor_tensor(out=bu[:], in0=b[:], in1=u[:], op=ALU.mult)
+            for h in range(2):
+                nc.vector.tensor_tensor(
+                    out=bv[:, half_cols(h)], in0=looked_up(b, l_n9, h), in1=v[:, half_cols(h)], op=ALU.mult
+                )
+            res = bu
+            nc.vector.scalar_tensor_tensor(
+                out=res[:], in0=bv[:], scalar=0.5, in1=bu[:], op0=ALU.mult, op1=ALU.add
+            )
+            nc.sync.dma_start(out=out[t * P : (t + 1) * P, :], in_=res[:])

@@ -19,6 +19,7 @@ P = 128
 PACK = 4
 HALF = S // 2
 LIST_COLS = S // 16
+SPARE = 8
 
 
 def tile_picked_tfcdflowbdetcmp_none_p_kernel(
@@ -38,11 +39,13 @@ def tile_picked_tfcdflowbdetcmp_none_p_kernel(
         def plane(name):
             return keep.tile([P, S], F32, name=name, align_bytes=64)
 
-        def half_cols(h):
-            return slice(h * HALF, (h + 1) * HALF)
+        def window(name):
+            tile = keep.tile([P, S + SPARE], F32, name=name, align_bytes=64)
+            nc.gpsimd.memset(tile[:, S:], 0.0)
+            return tile
 
-        def looked_up(window, lst, h):
-            return window[:].indirect(lst[:, h * LIST_COLS // 2 : (h + 1) * LIST_COLS // 2])
+        def fetch(out_ap, win, lst):
+            nc.scalar.activation(out=out_ap, in_=win[:].indirect(lst[:]), func=ACT.Copy)
 
         scale_rows = keep.tile([P, T], U8, name="scale_rows", align_bytes=64)
         nc.vector.memset(scale_rows[:].bitcast(I32), 0)
@@ -52,19 +55,19 @@ def tile_picked_tfcdflowbdetcmp_none_p_kernel(
             )
         l_offs = load_list("l_offs", offs)
         l_two = load_list("l_two", two)
-        words = keep.tile([P, T], I32, name="words", align_bytes=64)
-        nc.sync.dma_start(out=words[:], in_=x_words[0].rearrange("p n t -> p (n t)").bitcast(I32))
         w1_raw = []
         for h in range(2):
             raw = keep.tile([P, PACK, H // 2], F32, name="w1_raw%d" % h, align_bytes=64)
             nc.sync.dma_start(out=raw[:], in_=w1.rearrange("(p j) c -> p j c", j=PACK)[:, :, h * 256 : (h + 1) * 256])
             w1_raw.append(raw)
+        words = keep.tile([P, T], I32, name="words", align_bytes=64)
+        nc.sync.dma_start(out=words[:], in_=x_words[0].rearrange("p n t -> p (n t)").bitcast(I32))
         l_n1 = load_list("l_n1", n1)
         l_n3 = load_list("l_n3", n3)
-        w2_raw = keep.tile([P, PACK, H], F32, name="w2_raw", align_bytes=64)
-        nc.sync.dma_start(out=w2_raw[:], in_=w2.rearrange("(p j) c -> p j c", j=PACK))
         gn_sb = keep.tile([P, PACK], F32, name="gn_sb")
         nc.sync.dma_start(out=gn_sb[:], in_=gn.rearrange("(p t) o -> p (t o)", t=PACK))
+        w2_raw = keep.tile([P, PACK, H], F32, name="w2_raw", align_bytes=64)
+        nc.sync.dma_start(out=w2_raw[:], in_=w2.rearrange("(p j) c -> p j c", j=PACK))
         l_n2 = load_list("l_n2", n2)
         l_n4 = load_list("l_n4", n4)
         l_cand = load_list("l_cand", cand)
@@ -79,8 +82,8 @@ def tile_picked_tfcdflowbdetcmp_none_p_kernel(
         l_n9 = load_list("l_n9", n9)
 
         def mx_tiles(name):
-            codes = keep.tile([P, S], U32, name=name + "_codes", align_bytes=64)
-            scales = keep.tile([P, S], U8, name=name + "_scales", align_bytes=64)
+            codes = keep.tile([P, S], U32, name=name + "_codes", tag=name + "_codes", align_bytes=64)
+            scales = keep.tile([P, S], U8, name=name + "_scales", tag=name + "_scales", align_bytes=64)
             return codes, scales
 
         def pick_bytes(name, lst, tag):
@@ -88,8 +91,8 @@ def tile_picked_tfcdflowbdetcmp_none_p_kernel(
             nc.vector.tensor_copy(out=picked[:], in_=scale_rows[:].indirect(lst[:]))
             return picked
 
-        def pick_words(name, lst):
-            picked = keep.tile([P, S], U32, name=name, tag="picked_words", align_bytes=64)
+        def pick_words(name, lst, tag):
+            picked = keep.tile([P, S], U32, name=name, tag=tag, align_bytes=64)
             nc.vector.tensor_copy(out=picked[:], in_=words[:].bitcast(U32).indirect(lst[:]))
             return picked
 
@@ -112,18 +115,19 @@ def tile_picked_tfcdflowbdetcmp_none_p_kernel(
                 stop=True,
             )
 
-        def interleaved(grouped, h):
-            cols = slice(h * HALF * PACK, (h + 1) * HALF * PACK)
-            return grouped[:, cols].rearrange("p (c i t) -> p c t i", i=2, t=PACK)
+        def interleaved(grouped):
+            return grouped[:].rearrange("p (c i t) -> p c t i", i=2, t=PACK)
 
-        def by_pairs(planes, h):
-            return planes[:, :, half_cols(h)].rearrange("p t (c i) -> p c t i", i=2)
+        def by_pairs(planes):
+            return planes[:].rearrange("p t (c i) -> p c t i", i=2)
 
-        offs_bytes = pick_bytes("offs_bytes", l_offs, "picked_bytes")
-        x_offs = (pick_words("offs_words", l_offs), offs_bytes)
+        offs_bytes = pick_bytes("offs_bytes", l_offs, "offs_bytes")
         two_bytes = pick_bytes("two_bytes", l_two, "two_bytes")
+        x_offs = (pick_words("offs_words", l_offs, "offs_words"), offs_bytes)
 
         w1_g = keep.tile([P, PACK * H], BF16, name="w1_g", align_bytes=64)
+        warm = keep.tile([P, 1], F32, name="warm")
+        nc.scalar.activation(out=warm[:], in_=w1_raw[0][:, 0, 0:1], func=ACT.Sigmoid)
         for h in range(2):
             nc.scalar.copy(
                 out=w1_g[:].rearrange("p (t m j) -> p m j t", t=PACK, j=PACK)[:, h * 64 : (h + 1) * 64],
@@ -132,41 +136,41 @@ def tile_picked_tfcdflowbdetcmp_none_p_kernel(
         w1_q = mx_tiles("w1")
         y_banks = []
         for t in range(PACK):
-            quantize(w1_q, w1_g, t * P, P)
+            if t % 2 == 0:
+                quantize(w1_q, w1_g, t * P, 2 * P)
             bank = psum.tile([P, S], F32, name="y_bank%d" % t, tag="ya%d" % t)
             product(bank, w1_q, t, x_offs)
             y_banks.append(bank)
 
-        x_two = (pick_words("two_words", l_two), two_bytes)
-        cand_bytes = pick_bytes("cand_bytes", l_cand, "picked_bytes")
+        x_two = (pick_words("two_words", l_two, "two_words"), two_bytes)
 
+        d_windows = []
+        gain = keep.tile([P, PACK], F32, name="gain")
+        nc.vector.tensor_scalar(out=gain[:], in0=gn_sb[:], scalar1=0.75, scalar2=None, op0=ALU.mult)
         prod12 = keep.tile([P, PACK, S], F32, name="prod12", align_bytes=64)
         prod34 = keep.tile([P, PACK, S], F32, name="prod34", align_bytes=64)
         w2_g = keep.tile([P, PACK * H], BF16, name="w2_g", align_bytes=64)
         w2_q = mx_tiles("w2")
         d_banks = []
         for t in range(PACK):
-            y = plane("y%d" % t)
-            nc.scalar.copy(out=y[:], in_=y_banks[t][:])
-            yg = plane("yg%d" % t)
-            nc.vector.tensor_scalar(
-                out=yg[:], in0=y[:], scalar1=gn_sb[:, t : t + 1], scalar2=0.75, op0=ALU.mult, op1=ALU.mult
-            )
-            y1, y3 = plane("y1_%d" % t), plane("y3_%d" % t)
-            for h in range(2):
-                nc.scalar.activation(out=y1[:, half_cols(h)], in_=looked_up(y, l_n1, h), func=ACT.Copy)
-            for h in range(2):
-                nc.scalar.activation(out=y3[:, half_cols(h)], in_=looked_up(y, l_n3, h), func=ACT.Copy)
-            for h in range(2):
-                nc.vector.tensor_tensor(
-                    out=prod12[:, t, half_cols(h)], in0=looked_up(yg, l_n2, h), in1=y1[:, half_cols(h)], op=ALU.mult
+            y, yg = window("y%d" % t), window("yg%d" % t)
+            if t == 1:
+                nc.vector.tensor_copy(out=y[:, :S], in_=y_banks[t][:])
+                nc.scalar.activation(out=yg[:, :S], in_=y_banks[t][:], func=ACT.Copy, scale=gain[:, t : t + 1])
+            else:
+                nc.scalar.copy(out=y[:, :S], in_=y_banks[t][:])
+                nc.vector.tensor_scalar(
+                    out=yg[:, :S], in0=y[:, :S], scalar1=gain[:, t : t + 1], scalar2=None, op0=ALU.mult
                 )
-            for h in range(2):
-                nc.vector.tensor_tensor(
-                    out=prod34[:, t, half_cols(h)], in0=looked_up(yg, l_n4, h), in1=y3[:, half_cols(h)], op=ALU.mult
-                )
+            wide = keep.tile([P, 2 * S], F32, name="d_and_y1_%d" % t, align_bytes=64)
+            d_windows.append(wide)
+            y1, y3 = wide[:, S:], plane("y3_%d" % t)
+            fetch(y1, y, l_n1)
+            fetch(y3[:], y, l_n3)
+            nc.vector.tensor_tensor(out=prod12[:, t, :], in0=yg[:].indirect(l_n2[:]), in1=y1, op=ALU.mult)
+            nc.vector.tensor_tensor(out=prod34[:, t, :], in0=yg[:].indirect(l_n4[:]), in1=y3[:], op=ALU.mult)
             if t == 0:
-                nc.scalar.copy(
+                nc.vector.tensor_copy(
                     out=w2_g[:].rearrange("p (t m j) -> p m j t", t=PACK, j=PACK),
                     in_=w2_raw[:].rearrange("p j (m t) -> p m j t", t=PACK),
                 )
@@ -175,7 +179,6 @@ def tile_picked_tfcdflowbdetcmp_none_p_kernel(
                     bank = psum.tile([P, S], F32, name="d_bank%d" % td, tag="db%d" % td)
                     product(bank, w2_q, td, x_two)
                     d_banks.append(bank)
-                x_cand = (pick_words("cand_words", l_cand), cand_bytes)
 
         w3_g = keep.tile([P, PACK * N], BF16, name="w3_g", align_bytes=64)
         nc.vector.tensor_copy(
@@ -183,10 +186,7 @@ def tile_picked_tfcdflowbdetcmp_none_p_kernel(
             in_=w3_raw[:].rearrange("p j (c i) -> p c j i", i=4),
         )
         z_g = keep.tile([P, PACK * S], BF16, name="z_g", align_bytes=64)
-        for h in range(2):
-            nc.vector.tensor_tensor(
-                out=interleaved(z_g, h), in0=by_pairs(prod12, h), in1=by_pairs(prod34, h), op=ALU.subtract
-            )
+        nc.vector.tensor_tensor(out=interleaved(z_g), in0=by_pairs(prod12), in1=by_pairs(prod34), op=ALU.subtract)
         w3_q = mx_tiles("w3")
         quantize(w3_q, w3_g, 0, N)
         z_q = mx_tiles("z")
@@ -200,23 +200,17 @@ def tile_picked_tfcdflowbdetcmp_none_p_kernel(
         dg = keep.tile([P, PACK, S], F32, name="dg", align_bytes=64)
         gate = keep.tile([P, PACK, S], F32, name="gate", align_bytes=64)
         for t in range(PACK):
-            d = plane("d%d" % t)
-            nc.scalar.copy(out=d[:], in_=d_banks[t][:])
+            d = d_windows[t]
+            nc.scalar.copy(out=d[:, :S], in_=d_banks[t][:])
             d5 = plane("d5_%d" % t)
-            for h in range(2):
-                nc.scalar.activation(out=d5[:, half_cols(h)], in_=looked_up(d, l_n5, h), func=ACT.Copy)
-            nc.vector.tensor_scalar(
-                out=dg[:, t, :], in0=d[:], scalar1=gs_sb[:, t : t + 1], scalar2=None, op0=ALU.mult
-            )
+            fetch(d5[:], d, l_n5)
+            nc.scalar.activation(out=dg[:, t, :], in_=d_banks[t][:], func=ACT.Copy, scale=gs_sb[:, t : t + 1])
             back = plane("back%d" % t)
-            for h in range(2):
-                nc.vector.tensor_tensor(
-                    out=back[:, half_cols(h)], in0=looked_up(d, l_n6, h), in1=d5[:, half_cols(h)], op=ALU.subtract
-                )
+            nc.vector.tensor_tensor(out=back[:], in0=d[:].indirect(l_n6[:]), in1=d5[:], op=ALU.subtract)
             nc.scalar.activation(out=gate[:, t, :], in_=back[:], func=ACT.Sigmoid, scale=-1.0)
+        x_cand = (pick_words("cand_words", l_cand, "z_codes"), pick_bytes("cand_bytes", l_cand, "z_scales"))
         z2_g = keep.tile([P, PACK * S], BF16, name="z2_g", align_bytes=64)
-        for h in range(2):
-            nc.vector.tensor_tensor(out=interleaved(z2_g, h), in0=by_pairs(dg, h), in1=by_pairs(gate, h), op=ALU.mult)
+        nc.vector.tensor_tensor(out=interleaved(z2_g), in0=by_pairs(dg), in1=by_pairs(gate), op=ALU.mult)
         z2_q = mx_tiles("z2")
         quantize(z2_q, z2_g, 0, S)
         b_banks = []
@@ -226,26 +220,31 @@ def tile_picked_tfcdflowbdetcmp_none_p_kernel(
             b_banks.append(bank)
 
         for t in range(PACK):
-            a = plane("a%d" % t)
-            nc.scalar.copy(out=a[:], in_=a_banks[t][:])
-            a7, a8 = plane("a7_%d" % t), plane("a8_%d" % t)
-            for h in range(2):
-                nc.scalar.activation(out=a7[:, half_cols(h)], in_=looked_up(a, l_n7, h), func=ACT.Copy)
-            for h in range(2):
-                nc.scalar.activation(out=a8[:, half_cols(h)], in_=looked_up(a, l_n8, h), func=ACT.Copy)
-            b = plane("b%d" % t)
-            nc.scalar.activation(out=b[:], in_=b_banks[t][:], func=ACT.Copy, scale=0.0625)
-            u, v = a7, a8
-            nc.vector.tensor_tensor(out=u[:], in0=a7[:], in1=a[:], op=ALU.subtract)
-            nc.vector.tensor_tensor(out=v[:], in0=a8[:], in1=a[:], op=ALU.subtract)
-            bu, bv = plane("bu%d" % t), plane("bv%d" % t)
-            nc.vector.tensor_tensor(out=bu[:], in0=b[:], in1=u[:], op=ALU.mult)
-            for h in range(2):
-                nc.vector.tensor_tensor(
-                    out=bv[:, half_cols(h)], in0=looked_up(b, l_n9, h), in1=v[:, half_cols(h)], op=ALU.mult
+            a = window("a%d" % t)
+            nc.scalar.copy(out=a[:, :S], in_=a_banks[t][:])
+            u, v = plane("u%d" % t), plane("v%d" % t)
+            fetch(u[:], a, l_n7)
+            fetch(v[:], a, l_n8)
+            nc.vector.tensor_tensor(out=u[:], in0=u[:], in1=a[:, :S], op=ALU.subtract)
+            nc.vector.tensor_tensor(out=v[:], in0=v[:], in1=a[:, :S], op=ALU.subtract)
+            b = window("b%d" % t)
+            if t == 0:
+                nc.vector.tensor_scalar(
+                    out=b[:, :S], in0=b_banks[t][:], scalar1=0.0625, scalar2=None, op0=ALU.mult
                 )
-            res = bu
-            nc.vector.scalar_tensor_tensor(
-                out=res[:], in0=bv[:], scalar=0.5, in1=bu[:], op0=ALU.mult, op1=ALU.add
-            )
-            nc.sync.dma_start(out=out[t * P : (t + 1) * P, :], in_=res[:])
+            else:
+                nc.scalar.activation(out=b[:, :S], in_=b_banks[t][:], func=ACT.Copy, scale=0.0625)
+            bu, bv = plane("bu%d" % t), plane("bv%d" % t)
+            nc.vector.tensor_tensor(out=bu[:], in0=b[:, :S], in1=u[:], op=ALU.mult)
+            if t < 2:
+                nc.vector.tensor_tensor(out=bv[:], in0=b[:].indirect(l_n9[:]), in1=v[:], op=ALU.mult)
+            else:
+                fetch(bv[:], b, l_n9)
+                nc.vector.tensor_tensor(out=bv[:], in0=bv[:], in1=v[:], op=ALU.mult)
+            pieces = 2 if t == PACK - 1 else 1
+            for h in range(pieces):
+                cols = slice(h * S // pieces, (h + 1) * S // pieces)
+                nc.vector.scalar_tensor_tensor(
+                    out=bu[:, cols], in0=bv[:, cols], scalar=0.5, in1=bu[:, cols], op0=ALU.mult, op1=ALU.add
+                )
+                nc.sync.dma_start(out=out[t * P : (t + 1) * P, cols], in_=bu[:, cols])

from contextlib import ExitStack

import concourse.mybir as mybir

K, T, S, N, H, C = 512, 2048, 512, 512, 512, 512
FLOPS = 4 * 2 * 512 * 512 * 512

F32 = mybir.dt.float32
BF16 = mybir.dt.bfloat16
I32 = mybir.dt.int32
U32 = mybir.dt.uint32
U16 = mybir.dt.uint16
U8 = mybir.dt.uint8
FP8X4 = mybir.dt.float8_e4m3fn_x4
ALU = mybir.AluOpType
ACT = mybir.ActivationFunctionType

P = 128
PACK = 4
HALF = S // 2
LIST_COLS = S // 16
SPARE = 8


def tile_picked_tfcdflowbdetcmp_none_p_kernel(
    tc, x_words, x_scales, w1, w2, gn, w3, gs, offs, two, n1, n2, n3, n4, n5, n6, cand, n7, n8, n9, out
):
    nc = tc.nc
    with ExitStack() as ctx:
        lists = ctx.enter_context(tc.tile_pool(name="lists", bufs=1))
        keep = ctx.enter_context(tc.tile_pool(name="keep", bufs=1))
        psum = ctx.enter_context(tc.psum_pool(name="psum", bufs=1))

        def load_list(name, src):
            tile = lists.tile([P, LIST_COLS], U16, name=name)
            nc.sync.dma_start(tile[:], src)
            return tile

        def plane(name):
            return keep.tile([P, S], F32, name=name, align_bytes=64)

        def window(name):
            tile = keep.tile([P, S + SPARE], F32, name=name, align_bytes=64)
            nc.gpsimd.memset(tile[:, S:], 0.0)
            return tile

        def fetch(out_ap, win, lst):
            nc.scalar.activation(out=out_ap, in_=win[:].indirect(lst[:]), func=ACT.Copy)

        scale_rows = keep.tile([P, T], U8, name="scale_rows", align_bytes=64)
        nc.vector.memset(scale_rows[:].bitcast(I32), 0)
        for q in range(4):
            nc.scalar.dma_start(
                out=scale_rows[32 * q : 32 * q + 4, :].bitcast(I32), in_=x_scales[0, 4 * q : 4 * q + 4, :].bitcast(I32)
            )
        l_offs = load_list("l_offs", offs)
        l_two = load_list("l_two", two)
        w1_raw = []
        for h in range(2):
            raw = keep.tile([P, PACK, H // 2], F32, name="w1_raw%d" % h, align_bytes=64)
            nc.sync.dma_start(out=raw[:], in_=w1.rearrange("(p j) c -> p j c", j=PACK)[:, :, h * 256 : (h + 1) * 256])
            w1_raw.append(raw)
        words = keep.tile([P, T], I32, name="words", align_bytes=64)
        nc.sync.dma_start(out=words[:], in_=x_words[0].rearrange("p n t -> p (n t)").bitcast(I32))
        l_n1 = load_list("l_n1", n1)
        l_n3 = load_list("l_n3", n3)
        gn_sb = keep.tile([P, PACK], F32, name="gn_sb")
        nc.sync.dma_start(out=gn_sb[:], in_=gn.rearrange("(p t) o -> p (t o)", t=PACK))
        w2_raw = keep.tile([P, PACK, H], F32, name="w2_raw", align_bytes=64)
        nc.sync.dma_start(out=w2_raw[:], in_=w2.rearrange("(p j) c -> p j c", j=PACK))
        l_n2 = load_list("l_n2", n2)
        l_n4 = load_list("l_n4", n4)
        l_cand = load_list("l_cand", cand)
        w3_raw = keep.tile([P, PACK, N], F32, name="w3_raw", align_bytes=64)
        nc.sync.dma_start(out=w3_raw[:], in_=w3.rearrange("(p j) c -> p j c", j=PACK))
        l_n5 = load_list("l_n5", n5)
        l_n6 = load_list("l_n6", n6)
        gs_sb = keep.tile([P, PACK], F32, name="gs_sb")
        nc.sync.dma_start(out=gs_sb[:], in_=gs.rearrange("(p t) o -> p (t o)", t=PACK))
        l_n7 = load_list("l_n7", n7)
        l_n8 = load_list("l_n8", n8)
        l_n9 = load_list("l_n9", n9)

        def mx_tiles(name):
            codes = keep.tile([P, S], U32, name=name + "_codes", tag=name + "_codes", align_bytes=64)
            scales = keep.tile([P, S], U8, name=name + "_scales", tag=name + "_scales", align_bytes=64)
            return codes, scales

        def pick_bytes(name, lst, tag):
            picked = keep.tile([P, S], U8, name=name, tag=tag, align_bytes=64)
            nc.vector.tensor_copy(out=picked[:], in_=scale_rows[:].indirect(lst[:]))
            return picked

        def pick_words(name, lst, tag):
            picked = keep.tile([P, S], U32, name=name, tag=tag, align_bytes=64)
            nc.vector.tensor_copy(out=picked[:], in_=words[:].bitcast(U32).indirect(lst[:]))
            return picked

        def quantize(operand, grouped, first, count):
            nc.vector.quantize_mx(
                out=operand[0][:, first : first + count].bitcast(FP8X4),
                scales=operand[1][:, first : first + count],
                in_=grouped[:, PACK * first : PACK * (first + count)],
            )

        def product(bank, stationary, t, moving):
            cols = slice(t * P, (t + 1) * P)
            nc.tensor.matmul_mx(
                out=bank[:],
                lhsT=stationary[0][:, cols].bitcast(FP8X4),
                lhsT_scale=stationary[1][:, cols],
                rhs=moving[0][:].bitcast(FP8X4),
                rhs_scale=moving[1][:],
                start=True,
                stop=True,
            )

        def interleaved(grouped):
            return grouped[:].rearrange("p (c i t) -> p c t i", i=2, t=PACK)

        def by_pairs(planes):
            return planes[:].rearrange("p t (c i) -> p c t i", i=2)

        offs_bytes = pick_bytes("offs_bytes", l_offs, "offs_bytes")
        two_bytes = pick_bytes("two_bytes", l_two, "two_bytes")
        x_offs = (pick_words("offs_words", l_offs, "offs_words"), offs_bytes)

        w1_g = keep.tile([P, PACK * H], BF16, name="w1_g", align_bytes=64)
        warm = keep.tile([P, 1], F32, name="warm")
        nc.scalar.activation(out=warm[:], in_=w1_raw[0][:, 0, 0:1], func=ACT.Sigmoid)
        for h in range(2):
            nc.scalar.copy(
                out=w1_g[:].rearrange("p (t m j) -> p m j t", t=PACK, j=PACK)[:, h * 64 : (h + 1) * 64],
                in_=w1_raw[h][:].rearrange("p j (m t) -> p m j t", t=PACK),
            )
        w1_q = mx_tiles("w1")
        y_banks = []
        for t in range(PACK):
            if t % 2 == 0:
                quantize(w1_q, w1_g, t * P, 2 * P)
            bank = psum.tile([P, S], F32, name="y_bank%d" % t, tag="ya%d" % t)
            product(bank, w1_q, t, x_offs)
            y_banks.append(bank)

        x_two = (pick_words("two_words", l_two, "two_words"), two_bytes)

        d_windows = []
        gain = keep.tile([P, PACK], F32, name="gain")
        nc.vector.tensor_scalar(out=gain[:], in0=gn_sb[:], scalar1=0.75, scalar2=None, op0=ALU.mult)
        prod12 = keep.tile([P, PACK, S], F32, name="prod12", align_bytes=64)
        prod34 = keep.tile([P, PACK, S], F32, name="prod34", align_bytes=64)
        w2_g = keep.tile([P, PACK * H], BF16, name="w2_g", align_bytes=64)
        w2_q = mx_tiles("w2")
        d_banks = []
        for t in range(PACK):
            y, yg = window("y%d" % t), window("yg%d" % t)
            if t == 1:
                nc.vector.tensor_copy(out=y[:, :S], in_=y_banks[t][:])
                nc.scalar.activation(out=yg[:, :S], in_=y_banks[t][:], func=ACT.Copy, scale=gain[:, t : t + 1])
            else:
                nc.scalar.copy(out=y[:, :S], in_=y_banks[t][:])
                nc.vector.tensor_scalar(
                    out=yg[:, :S], in0=y[:, :S], scalar1=gain[:, t : t + 1], scalar2=None, op0=ALU.mult
                )
            wide = keep.tile([P, 2 * S], F32, name="d_and_y1_%d" % t, align_bytes=64)
            d_windows.append(wide)
            y1, y3 = wide[:, S:], plane("y3_%d" % t)
            fetch(y1, y, l_n1)
            fetch(y3[:], y, l_n3)
            nc.vector.tensor_tensor(out=prod12[:, t, :], in0=yg[:].indirect(l_n2[:]), in1=y1, op=ALU.mult)
            nc.vector.tensor_tensor(out=prod34[:, t, :], in0=yg[:].indirect(l_n4[:]), in1=y3[:], op=ALU.mult)
            if t == 0:
                nc.vector.tensor_copy(
                    out=w2_g[:].rearrange("p (t m j) -> p m j t", t=PACK, j=PACK),
                    in_=w2_raw[:].rearrange("p j (m t) -> p m j t", t=PACK),
                )
                quantize(w2_q, w2_g, 0, H)
                for td in range(PACK):
                    bank = psum.tile([P, S], F32, name="d_bank%d" % td, tag="db%d" % td)
                    product(bank, w2_q, td, x_two)
                    d_banks.append(bank)

        w3_g = keep.tile([P, PACK * N], BF16, name="w3_g", align_bytes=64)
        nc.vector.tensor_copy(
            out=w3_g[:].rearrange("p (c i j) -> p c j i", i=4, j=PACK),
            in_=w3_raw[:].rearrange("p j (c i) -> p c j i", i=4),
        )
        z_g = keep.tile([P, PACK * S], BF16, name="z_g", align_bytes=64)
        nc.vector.tensor_tensor(out=interleaved(z_g), in0=by_pairs(prod12), in1=by_pairs(prod34), op=ALU.subtract)
        w3_q = mx_tiles("w3")
        quantize(w3_q, w3_g, 0, N)
        z_q = mx_tiles("z")
        quantize(z_q, z_g, 0, S)
        a_banks = []
        for t in range(PACK):
            bank = psum.tile([P, S], F32, name="a_bank%d" % t, tag="ya%d" % t)
            product(bank, w3_q, t, z_q)
            a_banks.append(bank)

        dg = keep.tile([P, PACK, S], F32, name="dg", align_bytes=64)
        gate = keep.tile([P, PACK, S], F32, name="gate", align_bytes=64)
        for t in range(PACK):
            d = d_windows[t]
            nc.scalar.copy(out=d[:, :S], in_=d_banks[t][:])
            d5 = plane("d5_%d" % t)
            fetch(d5[:], d, l_n5)
            nc.scalar.activation(out=dg[:, t, :], in_=d_banks[t][:], func=ACT.Copy, scale=gs_sb[:, t : t + 1])
            back = plane("back%d" % t)
            nc.vector.tensor_tensor(out=back[:], in0=d[:].indirect(l_n6[:]), in1=d5[:], op=ALU.subtract)
            nc.scalar.activation(out=gate[:, t, :], in_=back[:], func=ACT.Sigmoid, scale=-1.0)
        x_cand = (pick_words("cand_words", l_cand, "z_codes"), pick_bytes("cand_bytes", l_cand, "z_scales"))
        z2_g = keep.tile([P, PACK * S], BF16, name="z2_g", align_bytes=64)
        nc.vector.tensor_tensor(out=interleaved(z2_g), in0=by_pairs(dg), in1=by_pairs(gate), op=ALU.mult)
        z2_q = mx_tiles("z2")
        quantize(z2_q, z2_g, 0, S)
        b_banks = []
        for t in range(PACK):
            bank = psum.tile([P, S], F32, name="b_bank%d" % t, tag="db%d" % t)
            product(bank, x_cand, t, z2_q)
            b_banks.append(bank)

        for t in range(PACK):
            a = window("a%d" % t)
            nc.scalar.copy(out=a[:, :S], in_=a_banks[t][:])
            u, v = plane("u%d" % t), plane("v%d" % t)
            fetch(u[:], a, l_n7)
            fetch(v[:], a, l_n8)
            nc.vector.tensor_tensor(out=u[:], in0=u[:], in1=a[:, :S], op=ALU.subtract)
            nc.vector.tensor_tensor(out=v[:], in0=v[:], in1=a[:, :S], op=ALU.subtract)
            b = window("b%d" % t)
            if t == 0:
                nc.vector.tensor_scalar(
                    out=b[:, :S], in0=b_banks[t][:], scalar1=0.0625, scalar2=None, op0=ALU.mult
                )
            else:
                nc.scalar.activation(out=b[:, :S], in_=b_banks[t][:], func=ACT.Copy, scale=0.0625)
            bu, bv = plane("bu%d" % t), plane("bv%d" % t)
            nc.vector.tensor_tensor(out=bu[:], in0=b[:, :S], in1=u[:], op=ALU.mult)
            if t < 2:
                nc.vector.tensor_tensor(out=bv[:], in0=b[:].indirect(l_n9[:]), in1=v[:], op=ALU.mult)
            else:
                fetch(bv[:], b, l_n9)
                nc.vector.tensor_tensor(out=bv[:], in0=bv[:], in1=v[:], op=ALU.mult)
            pieces = 2 if t == PACK - 1 else 1
            for h in range(pieces):
                cols = slice(h * S // pieces, (h + 1) * S // pieces)
                nc.vector.scalar_tensor_tensor(
                    out=bu[:, cols], in0=bv[:, cols], scalar=0.5, in1=bu[:, cols], op0=ALU.mult, op1=ALU.add
                )
                nc.sync.dma_start(out=out[t * P : (t + 1) * P, cols], in_=bu[:, cols])
